import numpy as np
import ml_dtypes


def mxq(x, axis, fmt="e4m3"):
    dtype, down = {"e4m3": (ml_dtypes.float8_e4m3fn, 7), "e5m2": (ml_dtypes.float8_e5m2, 14)}[fmt]
    v = np.moveaxis(np.asarray(x, np.float32).astype(ml_dtypes.bfloat16).astype(np.float64), axis, -1)
    blocks = v.reshape(v.shape[:-1] + (-1, 32))
    amax = np.abs(blocks).max(-1, keepdims=True)
    byte = np.maximum(np.where(amax > 0, np.frexp(amax)[1] - 1 + 127, 0) - down, 1)
    scale = np.exp2(byte - 127.0)
    codes = (blocks / scale).astype(np.float32).astype(dtype).astype(np.float64)
    return np.moveaxis((codes * scale).reshape(v.shape), -1, axis)


WIDE = False


def mx_kscale(k):
    if not WIDE:
        return np.ones(k)
    levels = np.array([10, -10, 5, -5, 0])
    if k % 512:
        return np.exp2(np.random.permutation(np.resize(levels, k // 32))).repeat(32)
    a = np.empty((k // 512, 16))
    for p in range(k // 512):
        a[p, :8] = np.random.permutation(np.resize(levels, 8))
        for g in range(8):
            far = levels[np.abs(levels - a[p, g]) >= 10]
            a[p, g + 8] = far[np.random.randint(len(far))]
    return np.exp2(a.ravel()).repeat(32)


def f64(x):
    return np.asarray(x).astype(np.float64)


def striped(idx):
    return np.tile(idx.reshape(-1, 16).T, (8, 1)).astype(np.uint16)


def unstriped(offs):
    return offs[:16].T.reshape(-1).astype(np.int64)


E2M1 = np.array([0.0, 0.5, 1.0, 1.5, 2.0, 3.0, 4.0, 6.0, -0.0, -0.5, -1.0, -1.5, -2.0, -3.0, -4.0, -6.0])


def pack_weight(w, fmt):
    k, n = w.shape
    w = f64(np.asarray(w, np.float32).astype(ml_dtypes.bfloat16)).reshape(k // 32, 32, n)
    amax = np.abs(w).max(1)
    if fmt == "e4m3":
        byte = np.frexp(amax)[1] - 1 + 127 - 7
    else:
        mant, ex = np.frexp(amax / 6.0)
        byte = np.where(mant > 0.5, ex, ex - 1) + 127
    byte = np.clip(np.where(amax > 0, byte, 1), 1, 254)
    scaled = (w * np.exp2(127.0 - byte)[:, None, :]).reshape(k, n).astype(np.float32)
    by_word = np.ascontiguousarray(scaled.reshape(k // 512, 128, 4, n).transpose(0, 1, 3, 2))
    if fmt == "e4m3":
        words = by_word.astype(ml_dtypes.float8_e4m3fn).view(np.uint8)
    else:
        c = by_word.astype(ml_dtypes.float4_e2m1fn).view(np.uint8) & 0xF
        words = (c[..., 0::2] | (c[..., 1::2] << 4)).reshape(k // 512, 128, 2 * n)
    return np.ascontiguousarray(words), np.ascontiguousarray(byte.astype(np.uint8).reshape(k // 512, 16, n))


def unpack_weight(words, scales, fmt):
    g, _, n = scales.shape
    words = np.ascontiguousarray(words).reshape(g, 128, n, -1)
    if fmt == "e4m3":
        vals = words.view(ml_dtypes.float8_e4m3fn).astype(np.float64)
    else:
        nib = np.empty((g, 128, n, 4), np.uint8)
        nib[..., 0::2] = words & 0xF
        nib[..., 1::2] = words >> 4
        vals = E2M1[nib]
    vals = vals * np.repeat(np.exp2(scales.astype(np.float64) - 127.0), 8, axis=1)[..., None]
    return vals.transpose(0, 1, 3, 2).reshape(g * 512, n)


def gelu(v):
    return 0.5 * v * (1.0 + np.tanh(np.sqrt(2.0 / np.pi) * (v + 0.044715 * v**3)))


K, H, T, S, T3, S2, P = 1024, 512, 4096, 1024, 2048, 1024, 512


def setup_inputs():
    n = np.random.standard_normal
    s = mx_kscale(K)[:, None]
    u = mx_kscale(H)[:, None]
    d = {}
    d["tab_words"], d["tab_scales"] = pack_weight(n((K, T)) * s, "e4m3")
    d["tab2_words"], d["tab2_scales"] = pack_weight(n((H, T3)) / u / H ** 0.5, "e4m3")
    d["offs"] = striped(np.random.permutation(T)[:S])
    d["offs2"] = striped(np.random.permutation(T3)[:S2])
    d["pos1"] = striped(np.random.permutation(S)[:P])
    d["pos2"] = striped(np.random.permutation(S)[:P])
    d["w1"] = (n((K, H)) / s * u.T / K ** 0.5).astype(np.float32)
    d["w4_words"], d["w4_scales"] = pack_weight(n((K, H)) / s * u.T / K ** 0.5, "e2m1")
    d["w8_words"], d["w8_scales"] = pack_weight(n((K, H)) / s * u.T / K ** 0.5, "e4m3")
    d["stand"] = n(S2).astype(np.float32)
    return d


def reference(tab_words, tab_scales, tab2_words, tab2_scales, offs, offs2, pos1, pos2,
              w1, w4_words, w4_scales, w8_words, w8_scales, stand):
    v = unpack_weight(tab_words, tab_scales, "e4m3")[:, unstriped(offs)]
    v2 = unpack_weight(tab2_words, tab2_scales, "e4m3")[:, unstriped(offs2)]
    a1 = mxq(f64(w1), 0, "e4m3").T @ v
    a2 = unpack_weight(w4_words, w4_scales, "e2m1").T @ v
    a3 = unpack_weight(w8_words, w8_scales, "e4m3").T @ v
    h = np.minimum(a1, a2) + np.maximum(a2, a3)
    e = v2.T @ mxq(h, 0, "e4m3")
    pod = np.abs(e[:, unstriped(pos1)] - f64(stand)[:, None])
    return np.maximum(pod, e[:, unstriped(pos2)])

@@ -1,0 +1,289 @@
+from contextlib import ExitStack
+
+import concourse.mybir as mybir
+from concourse.masks import make_identity
+
+K, H, T, S, T3, S2, NP = 1024, 512, 4096, 1024, 2048, 1024, 512
+FLOPS = 2 * (3 * K * H * S + H * S2 * S)
+
+F32 = mybir.dt.float32
+BF16 = mybir.dt.bfloat16
+I32 = mybir.dt.int32
+U32 = mybir.dt.uint32
+U16 = mybir.dt.uint16
+U8 = mybir.dt.uint8
+FP8X4 = mybir.dt.float8_e4m3fn_x4
+FP4X4 = mybir.dt.float4_e2m1fn_x4
+ALU = mybir.AluOpType
+ACT = mybir.ActivationFunctionType
+
+P = 128
+PASSES = K // 512
+TILES = S // P
+MT = S2 // P
+GP_ADDS = 4
+HELD_BACK = 2
+
+
+def tile_list_orchid_cross_scores_kernel(
+    tc, tab_words, tab_scales, tab2_words, tab2_scales, offs, offs2, pos1, pos2,
+    w1, w4_words, w4_scales, w8_words, w8_scales, stand, out,
+):
+    nc = tc.nc
+    with ExitStack() as ctx:
+        lists = ctx.enter_context(tc.tile_pool(name="lists", bufs=1))
+        keep = ctx.enter_context(tc.tile_pool(name="keep", bufs=1))
+        ring = ctx.enter_context(tc.tile_pool(name="ring", bufs=3))
+        psum = ctx.enter_context(tc.psum_pool(name="psum", bufs=8))
+
+        def held(name, shape, dtype):
+            return keep.tile(shape, dtype, name=name, align_bytes=64)
+
+        def bank(shape):
+            return psum.tile(shape, F32, name="bank")
+
+        offs_sb = lists.tile([P, S // 16], U16, name="offs_sb")
+        offs2_sb = lists.tile([P, S2 // 16], U16, name="offs2_sb")
+        pos1_sb = lists.tile([P, NP // 16], U16, name="pos1_sb")
+        pos2_sb = lists.tile([P, NP // 16], U16, name="pos2_sb")
+
+        tab_sb = [held("tab%d" % a, [P, T], I32) for a in range(PASSES)]
+        tabs_sb = held("tabs", [P, T], U8)
+        tab2_sb = held("tab2", [P, T3], I32)
+        tab2s_sb = held("tab2s", [P, T3], U8)
+        w4_sb = held("w4", [P, PASSES, 2 * H], U8)
+        w4s_sb = held("w4s", [P, PASSES, H], U8)
+        w8_sb = held("w8", [P, PASSES, H], I32)
+        w8s_sb = held("w8s", [P, PASSES, H], U8)
+        v_scales = [held("vs%d" % a, [P, S], U8) for a in range(PASSES)]
+        ident = held("ident", [P, P], F32)
+        stand_sb = held("stand_sb", [P, MT], F32)
+
+        for q in range(4):
+            eng = nc.vector if q < 2 else nc.gpsimd
+            eng.memset(tabs_sb[32 * q : 32 * q + 24, :].bitcast(I32), 0)
+        nc.vector.memset(w4s_sb[:].rearrange("p a c -> p (a c)").bitcast(I32), 0)
+        nc.gpsimd.memset(tab2s_sb[:].bitcast(I32), 0)
+        nc.vector.memset(w8s_sb[:].rearrange("p a c -> p (a c)").bitcast(I32), 0)
+        for a in range(PASSES):
+            nc.vector.memset(v_scales[a][:].bitcast(I32), 0)
+
+        def load_weight_scales(queue, dst, src):
+            for q in range(4):
+                queue.dma_start(
+                    out=dst[32 * q : 32 * q + 4, :, :].bitcast(I32),
+                    in_=src[:, 4 * q : 4 * q + 4, :].bitcast(I32).rearrange("a r c -> r a c"),
+                )
+
+        for q in range(4):
+            nc.gpsimd.dma_start(
+                out=tab2s_sb[32 * q : 32 * q + 4, :].bitcast(I32),
+                in_=tab2_scales[0, 4 * q : 4 * q + 4, :].bitcast(I32),
+            )
+        make_identity(nc, ident[:])
+
+        def load_words(dst, src):
+            nc.sync.dma_start(out=dst, in_=src.rearrange("p n i -> p (n i)").bitcast(I32))
+
+        half = H // 2
+        w1_raw = [held("w1raw%d" % c, [P, 4, half], F32) for c in range(2 * PASSES)]
+
+        def load_w1(c):
+            a, hc = divmod(c, 2)
+            nc.sync.dma_start(
+                out=w1_raw[c][:],
+                in_=w1[512 * a : 512 * (a + 1), hc * half : (hc + 1) * half].rearrange("(p i) c -> p i c", i=4),
+            )
+
+        nc.sync.dma_start(offs_sb[:], offs)
+        for q in range(4):
+            nc.sync.dma_start(
+                out=tabs_sb[32 * q + 24 : 32 * q + 32, :].bitcast(I32),
+                in_=tab_scales[:, 4 * q : 4 * q + 4, :].bitcast(I32),
+            )
+        load_words(tab_sb[0][:], tab_words[0])
+        nc.sync.dma_start(offs2_sb[:], offs2)
+        nc.sync.dma_start(out=w4_sb[:].bitcast(I32), in_=w4_words.bitcast(I32).rearrange("a p c -> p a c"))
+        load_weight_scales(nc.sync, w4s_sb, w4_scales)
+        load_words(tab_sb[1][:], tab_words[1])
+
+        vs_picked = held("vs_picked", [P, S], U8)
+        nc.vector.tensor_copy(vs_picked[:], tabs_sb[:].indirect(offs_sb[:]))
+        for a in range(PASSES):
+            nc.gpsimd.dma_start(
+                out=v_scales[a][0:100, :].bitcast(I32), in_=vs_picked[24 + 4 * a : 124 + 4 * a, :].bitcast(I32)
+            )
+
+        nc.sync.dma_start(
+            out=w8_sb[:], in_=w8_words.rearrange("a p c i -> p a (c i)").bitcast(I32)
+        )
+        load_weight_scales(nc.sync, w8s_sb, w8_scales)
+        for c in range(2 * PASSES):
+            load_w1(c)
+        load_words(tab2_sb[:], tab2_words[0])
+        nc.sync.dma_start(pos1_sb[:], pos1)
+        nc.sync.dma_start(pos2_sb[:], pos2)
+        with nc.allow_non_contiguous_dma(reason="one reference score a partition"):
+            nc.sync.dma_start(out=stand_sb[:], in_=stand.rearrange("(c p) -> p c", p=P))
+
+        v_words = [[held("v%d_%d" % (a, g), [P, 512], U32) for g in range(2)] for a in range(PASSES)]
+
+        def gather_v(a, g):
+            nc.vector.tensor_copy(
+                v_words[a][g][:], tab_sb[a][:].bitcast(U32).indirect(offs_sb[:, 32 * g : 32 * (g + 1)])
+            )
+
+        def first_stage(acc, j, a, rhs, rhs_scale):
+            g, c = divmod(j, 4)
+            nc.tensor.matmul_mx(
+                out=acc[:],
+                lhsT=v_words[a][g][:, P * c : P * (c + 1)].bitcast(FP8X4),
+                lhsT_scale=v_scales[a][:, P * j : P * (j + 1)],
+                rhs=rhs,
+                rhs_scale=rhs_scale,
+                start=(a == 0),
+                stop=(a == PASSES - 1),
+            )
+
+        def dealt(ap):
+            return ap.rearrange("p (m u e) -> p u m e", u=2, e=2)
+
+        def as_dealt(ap):
+            return ap.rearrange("p (u m e) -> p u m e", u=2, e=2)
+
+        gather_v(0, 0)
+        gather_v(0, 1)
+        v2_scales = held("v2s", [P, S2], U8)
+        nc.vector.tensor_copy(v2_scales[:], tab2s_sb[:].indirect(offs2_sb[:]))
+
+        a2_acc = [bank([P, H]) for j in range(TILES)]
+        for j in range(TILES):
+            first_stage(a2_acc[j], j, 0, w4_sb[:, 0, :].bitcast(FP4X4), w4s_sb[:, 0, :])
+        gather_v(1, 0)
+        gather_v(1, 1)
+        a2 = [held("a2_%d" % j, [P, H], F32) for j in range(TILES)]
+        for j in range(TILES):
+            first_stage(a2_acc[j], j, 1, w4_sb[:, 1, :].bitcast(FP4X4), w4s_sb[:, 1, :])
+            nc.scalar.copy(as_dealt(a2[j][:]), dealt(a2_acc[j][:]))
+
+        w1_bf = keep.tile([P, PASSES * H, 4], BF16, name="w1bf", tag="reused", align_bytes=64)
+        for c in range(2 * PASSES):
+            dst = w1_bf[:, c * half : (c + 1) * half, :]
+            src = w1_raw[c][:].rearrange("p i c -> p c i")
+            if c < 2 * PASSES - 1:
+                nc.gpsimd.tensor_scalar(dst, src, 1.0, 0.0, ALU.mult, ALU.add)
+            else:
+                nc.scalar.copy(dst, src)
+
+        def high(j, dst):
+            acc = bank([P, H])
+            for a in range(PASSES):
+                first_stage(acc, j, a, w8_sb[:, a, :].bitcast(FP8X4), w8s_sb[:, a, :])
+            nc.vector.tensor_tensor(as_dealt(dst), dealt(acc[:]), as_dealt(a2[j][:]), ALU.max)
+
+        hi = [held("hi_%d" % j, [P, H], F32)[:] for j in range(TILES - HELD_BACK)]
+        for j in range(TILES - HELD_BACK):
+            high(j, hi[j])
+
+        w1_codes = held("w1codes", [P, PASSES * H], U32)
+        w1_scales = held("w1scales", [P, PASSES * H], U8)
+        nc.vector.quantize_mx(
+            out=w1_codes[:].bitcast(FP8X4), scales=w1_scales[:], in_=w1_bf[:].rearrange("p c i -> p (c i)")
+        )
+        hi_late = keep.tile([P, HELD_BACK * H], F32, name="hi_late", tag="reused", align_bytes=64)
+        for n in range(HELD_BACK):
+            hi.append(hi_late[:, n * H : (n + 1) * H])
+            high(TILES - HELD_BACK + n, hi[-1])
+
+        v2_words = [held("v2w%d" % g, [P, 256], U32) for g in range(4)]
+
+        def gather_v2(g):
+            nc.vector.tensor_copy(
+                v2_words[g][:], tab2_sb[:].bitcast(U32).indirect(offs2_sb[:, 16 * g : 16 * (g + 1)])
+            )
+
+        chunks = [(0, 4), (4, 6), (6, 8)]
+        h_words = [held("hw%d" % lo, [P, (up - lo) * P * 2], F32) for lo, up in chunks]
+        h_codes = held("hcodes", [P, S], U32)
+        h_scales = held("hscales", [P, S], U8)
+
+        def low(j):
+            acc = bank([P, H])
+            for a in range(PASSES):
+                first_stage(acc, j, a, w1_codes[:, a * H : (a + 1) * H].bitcast(FP8X4), w1_scales[:, a * H : (a + 1) * H])
+            dst = ring.tile([P, H], F32, name="low", bufs=TILES)
+            nc.vector.tensor_tensor(as_dealt(dst[:]), dealt(acc[:]), as_dealt(a2[j][:]), ALU.min)
+            return dst
+
+        def add(j, eng):
+            ht = ring.tile([P, H], BF16, name="ht", bufs=TILES)
+            eng.tensor_tensor(ht[:], lows[j][:], hi[j], ALU.add)
+            return ht
+
+        def turn(j, ht):
+            words = ht[:].bitcast(F32)
+            turned = bank([P, 2, P])
+            for u in range(2):
+                nc.tensor.transpose(turned[:, u, :], words[:, P * u : P * (u + 1)], ident[:])
+            n = [c for c, (lo, up) in enumerate(chunks) if lo <= j < up][0]
+            lo, up = chunks[n]
+            dst = h_words[n][:, (j - lo) * 2 * P : (j - lo + 1) * 2 * P].rearrange("p (j u) -> p j u", u=2)
+            nc.scalar.copy(dst, turned[:].rearrange("p u j -> p j u"))
+            if j == up - 1:
+                nc.vector.quantize_mx(
+                    out=h_codes[:, lo * P : up * P].bitcast(FP8X4),
+                    scales=h_scales[:, lo * P : up * P],
+                    in_=h_words[n][:].bitcast(BF16),
+                )
+
+        lows = []
+        hts = []
+        for j in range(TILES):
+            lows.append(low(j))
+            if j < GP_ADDS:
+                hts.append(add(j, nc.gpsimd))
+            elif j > GP_ADDS:
+                hts.append(add(j - 1, nc.vector))
+        gather_v2(0)
+        hts.append(add(TILES - 1, nc.vector))
+        for j in range(TILES):
+            turn(j, hts[j])
+        for g in range(1, 4):
+            gather_v2(g)
+
+        def scores(i):
+            e = ring.tile([P, S], F32, name="e")
+            g, c = divmod(i, 2)
+            for n in range(2):
+                acc = bank([P, 512])
+                nc.tensor.matmul_mx(
+                    out=acc[:],
+                    lhsT=v2_words[g][:, P * c : P * (c + 1)].bitcast(FP8X4),
+                    lhsT_scale=v2_scales[:, P * i : P * (i + 1)],
+                    rhs=h_codes[:, 512 * n : 512 * (n + 1)].bitcast(FP8X4),
+                    rhs_scale=h_scales[:, 512 * n : 512 * (n + 1)],
+                    start=True,
+                    stop=True,
+                )
+                nc.scalar.copy(e[:, 512 * n : 512 * (n + 1)], acc[:])
+            return e
+
+        def pod_side(i, e):
+            picked = ring.tile([P, NP], F32, name="picked")
+            nc.vector.tensor_copy(picked[:], e[:].indirect(pos1_sb[:]))
+            pod = ring.tile([P, NP], F32, name="pod")
+            nc.scalar.activation(pod[:], picked[:], ACT.Abs, bias=stand_sb[:, i : i + 1], scale=-1.0)
+            return pod
+
+        es = [scores(0), scores(1)]
+        pods = [pod_side(0, es[0])]
+        for i in range(MT):
+            pollen = ring.tile([P, NP], F32, name="pollen")
+            nc.vector.tensor_copy(pollen[:], es[i][:].indirect(pos2_sb[:]))
+            if i + 2 < MT:
+                es.append(scores(i + 2))
+            if i + 1 < MT:
+                pods.append(pod_side(i + 1, es[i + 1]))
+            res = ring.tile([P, NP], F32, name="res")
+            nc.vector.tensor_tensor(res[:], pods[i][:], pollen[:], ALU.max)
+            nc.sync.dma_start(out=out[P * i : P * (i + 1), :], in_=res[:])

@@ -21,8 +21,8 @@ P = 128
 PASSES = K // 512
 TILES = S // P
 MT = S2 // P
-GP_ADDS = 4
-HELD_BACK = 2
+SUMMED_FIRST = (0, 1, 2, 7)
+HELD_BACK = (5, 6)
 
 
 def tile_list_orchid_cross_scores_kernel(
@@ -37,7 +37,7 @@ def tile_list_orchid_cross_scores_kernel(
         psum = ctx.enter_context(tc.psum_pool(name="psum", bufs=8))
 
         def held(name, shape, dtype):
-            return keep.tile(shape, dtype, name=name, align_bytes=64)
+            return keep.tile(shape, dtype, name=name, tag=name, align_bytes=64)
 
         def bank(shape):
             return psum.tile(shape, F32, name="bank")
@@ -59,14 +59,11 @@ def tile_list_orchid_cross_scores_kernel(
         ident = held("ident", [P, P], F32)
         stand_sb = held("stand_sb", [P, MT], F32)
 
+        nc.gpsimd.memset(w4s_sb[:].rearrange("p a c -> p (a c)").bitcast(I32), 0)
+        make_identity(nc, ident[:])
         for q in range(4):
-            eng = nc.vector if q < 2 else nc.gpsimd
-            eng.memset(tabs_sb[32 * q : 32 * q + 24, :].bitcast(I32), 0)
-        nc.vector.memset(w4s_sb[:].rearrange("p a c -> p (a c)").bitcast(I32), 0)
-        nc.gpsimd.memset(tab2s_sb[:].bitcast(I32), 0)
-        nc.vector.memset(w8s_sb[:].rearrange("p a c -> p (a c)").bitcast(I32), 0)
-        for a in range(PASSES):
-            nc.vector.memset(v_scales[a][:].bitcast(I32), 0)
+            nc.vector.memset(tabs_sb[32 * q : 32 * q + 24, :].bitcast(I32), 0)
+        nc.vector.memset(v_scales[0][:].bitcast(I32), 0)
 
         def load_weight_scales(queue, dst, src):
             for q in range(4):
@@ -74,13 +71,6 @@ def tile_list_orchid_cross_scores_kernel(
                     out=dst[32 * q : 32 * q + 4, :, :].bitcast(I32),
                     in_=src[:, 4 * q : 4 * q + 4, :].bitcast(I32).rearrange("a r c -> r a c"),
                 )
-
-        for q in range(4):
-            nc.gpsimd.dma_start(
-                out=tab2s_sb[32 * q : 32 * q + 4, :].bitcast(I32),
-                in_=tab2_scales[0, 4 * q : 4 * q + 4, :].bitcast(I32),
-            )
-        make_identity(nc, ident[:])
 
         def load_words(dst, src):
             nc.sync.dma_start(out=dst, in_=src.rearrange("p n i -> p (n i)").bitcast(I32))
@@ -101,18 +91,28 @@ def tile_list_orchid_cross_scores_kernel(
                 out=tabs_sb[32 * q + 24 : 32 * q + 32, :].bitcast(I32),
                 in_=tab_scales[:, 4 * q : 4 * q + 4, :].bitcast(I32),
             )
-        load_words(tab_sb[0][:], tab_words[0])
+        nc.sync.dma_start(out=tab2s_sb[16:32, :].bitcast(I32), in_=tab2_scales[0].bitcast(I32))
         nc.sync.dma_start(offs2_sb[:], offs2)
+        load_words(tab_sb[0][:], tab_words[0])
         nc.sync.dma_start(out=w4_sb[:].bitcast(I32), in_=w4_words.bitcast(I32).rearrange("a p c -> p a c"))
         load_weight_scales(nc.sync, w4s_sb, w4_scales)
-        load_words(tab_sb[1][:], tab_words[1])
 
         vs_picked = held("vs_picked", [P, S], U8)
         nc.vector.tensor_copy(vs_picked[:], tabs_sb[:].indirect(offs_sb[:]))
-        for a in range(PASSES):
-            nc.gpsimd.dma_start(
+
+        def shift(a):
+            nc.sync.dma_start(
                 out=v_scales[a][0:100, :].bitcast(I32), in_=vs_picked[24 + 4 * a : 124 + 4 * a, :].bitcast(I32)
             )
+
+        shift(0)
+        load_words(tab_sb[1][:], tab_words[1])
+        nc.vector.memset(v_scales[1][:].bitcast(I32), 0)
+        shift(1)
+
+        nc.vector.memset(w8s_sb[:].rearrange("p a c -> p (a c)").bitcast(I32), 0)
+        for lo, up in ((0, 16), (32, 64), (64, 128)):
+            nc.vector.memset(tab2s_sb[lo:up, :].bitcast(I32), 0)
 
         nc.sync.dma_start(
             out=w8_sb[:], in_=w8_words.rearrange("a p c i -> p a (c i)").bitcast(I32)
@@ -145,16 +145,20 @@ def tile_list_orchid_cross_scores_kernel(
                 stop=(a == PASSES - 1),
             )
 
-        def dealt(ap):
-            return ap.rearrange("p (m u e) -> p u m e", u=2, e=2)
+        def dealt(j, ap):
+            if j in SUMMED_FIRST:
+                return ap.rearrange("p (m u e) -> p u m e", u=2, e=2)
+            return ap.rearrange("p (m t) -> p t m", t=4)
 
-        def as_dealt(ap):
-            return ap.rearrange("p (u m e) -> p u m e", u=2, e=2)
+        def as_dealt(j, ap):
+            if j in SUMMED_FIRST:
+                return ap.rearrange("p (u m e) -> p u m e", u=2, e=2)
+            return ap.rearrange("p (t m) -> p t m", t=4)
 
         gather_v(0, 0)
         gather_v(0, 1)
-        v2_scales = held("v2s", [P, S2], U8)
-        nc.vector.tensor_copy(v2_scales[:], tab2s_sb[:].indirect(offs2_sb[:]))
+        v2s_picked = held("v2s_picked", [P, S2], U8)
+        nc.vector.tensor_copy(v2s_picked[:], tab2s_sb[:].indirect(offs2_sb[:]))
 
         a2_acc = [bank([P, H]) for j in range(TILES)]
         for j in range(TILES):
@@ -164,7 +168,7 @@ def tile_list_orchid_cross_scores_kernel(
         a2 = [held("a2_%d" % j, [P, H], F32) for j in range(TILES)]
         for j in range(TILES):
             first_stage(a2_acc[j], j, 1, w4_sb[:, 1, :].bitcast(FP4X4), w4s_sb[:, 1, :])
-            nc.scalar.copy(as_dealt(a2[j][:]), dealt(a2_acc[j][:]))
+            nc.scalar.copy(as_dealt(j, a2[j][:]), dealt(j, a2_acc[j][:]))
 
         w1_bf = keep.tile([P, PASSES * H, 4], BF16, name="w1bf", tag="reused", align_bytes=64)
         for c in range(2 * PASSES):
@@ -175,25 +179,42 @@ def tile_list_orchid_cross_scores_kernel(
             else:
                 nc.scalar.copy(dst, src)
 
-        def high(j, dst):
+        v2_scales = keep.tile([P, S2], U8, name="v2s", tag="w1raw3", align_bytes=64)
+        nc.gpsimd.memset(v2_scales[:].bitcast(I32), 0)
+        for q in range(4):
+            nc.sync.dma_start(
+                out=v2_scales[32 * q : 32 * q + 4, :].bitcast(I32),
+                in_=v2s_picked[16 + 4 * q : 20 + 4 * q, :].bitcast(I32),
+            )
+
+        def high_product(j):
             acc = bank([P, H])
             for a in range(PASSES):
                 first_stage(acc, j, a, w8_sb[:, a, :].bitcast(FP8X4), w8s_sb[:, a, :])
-            nc.vector.tensor_tensor(as_dealt(dst), dealt(acc[:]), as_dealt(a2[j][:]), ALU.max)
+            return acc
 
-        hi = [held("hi_%d" % j, [P, H], F32)[:] for j in range(TILES - HELD_BACK)]
-        for j in range(TILES - HELD_BACK):
-            high(j, hi[j])
+        def high_max(j, acc, dst):
+            nc.vector.tensor_tensor(as_dealt(j, dst), dealt(j, acc[:]), as_dealt(j, a2[j][:]), ALU.max)
+
+        def high(j, dst):
+            high_max(j, high_product(j), dst)
+
+        hi = {}
+        for j in range(TILES):
+            if j not in HELD_BACK:
+                hi[j] = held("hi_%d" % j, [P, H], F32)[:]
+                high(j, hi[j])
 
         w1_codes = held("w1codes", [P, PASSES * H], U32)
         w1_scales = held("w1scales", [P, PASSES * H], U8)
         nc.vector.quantize_mx(
             out=w1_codes[:].bitcast(FP8X4), scales=w1_scales[:], in_=w1_bf[:].rearrange("p c i -> p (c i)")
         )
-        hi_late = keep.tile([P, HELD_BACK * H], F32, name="hi_late", tag="reused", align_bytes=64)
-        for n in range(HELD_BACK):
-            hi.append(hi_late[:, n * H : (n + 1) * H])
-            high(TILES - HELD_BACK + n, hi[-1])
+        hi_late = keep.tile([P, len(HELD_BACK) * H], F32, name="hi_late", tag="reused", align_bytes=64)
+        for n, j in enumerate(HELD_BACK):
+            hi[j] = hi_late[:, n * H : (n + 1) * H]
+        late_acc = [high_product(j) for j in HELD_BACK]
+        high_max(HELD_BACK[0], late_acc[0], hi[HELD_BACK[0]])
 
         v2_words = [held("v2w%d" % g, [P, 256], U32) for g in range(4)]
 
@@ -202,8 +223,8 @@ def tile_list_orchid_cross_scores_kernel(
                 v2_words[g][:], tab2_sb[:].bitcast(U32).indirect(offs2_sb[:, 16 * g : 16 * (g + 1)])
             )
 
-        chunks = [(0, 4), (4, 6), (6, 8)]
-        h_words = [held("hw%d" % lo, [P, (up - lo) * P * 2], F32) for lo, up in chunks]
+        chunks = [(0, 4), (4, 6), (6, 7), (7, 8)]
+        h_bf = [held("hbf%d" % lo, [P, (up - lo) * H], BF16) for lo, up in chunks]
         h_codes = held("hcodes", [P, S], U32)
         h_scales = held("hscales", [P, S], U8)
 
@@ -212,60 +233,79 @@ def tile_list_orchid_cross_scores_kernel(
             for a in range(PASSES):
                 first_stage(acc, j, a, w1_codes[:, a * H : (a + 1) * H].bitcast(FP8X4), w1_scales[:, a * H : (a + 1) * H])
             dst = ring.tile([P, H], F32, name="low", bufs=TILES)
-            nc.vector.tensor_tensor(as_dealt(dst[:]), dealt(acc[:]), as_dealt(a2[j][:]), ALU.min)
+            nc.vector.tensor_tensor(as_dealt(j, dst[:]), dealt(j, acc[:]), as_dealt(j, a2[j][:]), ALU.min)
             return dst
 
-        def add(j, eng):
-            ht = ring.tile([P, H], BF16, name="ht", bufs=TILES)
-            eng.tensor_tensor(ht[:], lows[j][:], hi[j], ALU.add)
+        def add(j):
+            ht = ring.tile([P, H], BF16, name="ht", bufs=len(SUMMED_FIRST))
+            nc.gpsimd.tensor_tensor(ht[:], lows[j][:], hi[j], ALU.add)
             return ht
 
-        def turn(j, ht):
-            words = ht[:].bitcast(F32)
-            turned = bank([P, 2, P])
-            for u in range(2):
-                nc.tensor.transpose(turned[:, u, :], words[:, P * u : P * (u + 1)], ident[:])
+        done = []
+
+        def turn(j):
             n = [c for c, (lo, up) in enumerate(chunks) if lo <= j < up][0]
             lo, up = chunks[n]
-            dst = h_words[n][:, (j - lo) * 2 * P : (j - lo + 1) * 2 * P].rearrange("p (j u) -> p j u", u=2)
-            nc.scalar.copy(dst, turned[:].rearrange("p u j -> p j u"))
-            if j == up - 1:
+            dst = h_bf[n][:, (j - lo) * H : (j - lo + 1) * H]
+            if j in SUMMED_FIRST:
+                words = hts[j][:].bitcast(F32)
+                turned = bank([P, 2, P])
+                for u in range(2):
+                    nc.tensor.transpose(turned[:, u, :], words[:, P * u : P * (u + 1)], ident[:])
+                nc.scalar.copy(
+                    dst.bitcast(F32).rearrange("p (j u) -> p j u", u=2), turned[:].rearrange("p u j -> p j u")
+                )
+            else:
+                turned = bank([P, 4, P])
+                for t in range(4):
+                    cols = slice(P * t, P * (t + 1))
+                    nc.tensor.matmul(
+                        turned[:, t, :], hi[j][:, cols], ident[:], start=True, stop=False, is_transpose=True
+                    )
+                    nc.tensor.matmul(
+                        turned[:, t, :], lows[j][:, cols], ident[:], start=False, stop=True, is_transpose=True
+                    )
+                nc.scalar.copy(dst.rearrange("p (j t) -> p j t", t=4), turned[:].rearrange("p t j -> p j t"))
+            done.append(j)
+            if all(x in done for x in range(lo, up)):
                 nc.vector.quantize_mx(
                     out=h_codes[:, lo * P : up * P].bitcast(FP8X4),
                     scales=h_scales[:, lo * P : up * P],
-                    in_=h_words[n][:].bitcast(BF16),
+                    in_=h_bf[n][:],
                 )
 
-        lows = []
-        hts = []
+        lows = {}
+        hts = {}
+        for j in SUMMED_FIRST:
+            lows[j] = low(j)
+            hts[j] = add(j)
+        high_max(HELD_BACK[1], late_acc[1], hi[HELD_BACK[1]])
         for j in range(TILES):
-            lows.append(low(j))
-            if j < GP_ADDS:
-                hts.append(add(j, nc.gpsimd))
-            elif j > GP_ADDS:
-                hts.append(add(j - 1, nc.vector))
+            if j not in SUMMED_FIRST:
+                lows[j] = low(j)
         gather_v2(0)
-        hts.append(add(TILES - 1, nc.vector))
-        for j in range(TILES):
-            turn(j, hts[j])
+        for j in (0, 1, 3, 2, 4, 5, 6, 7):
+            turn(j)
         for g in range(1, 4):
             gather_v2(g)
 
         def scores(i):
             e = ring.tile([P, S], F32, name="e")
             g, c = divmod(i, 2)
-            for n in range(2):
-                acc = bank([P, 512])
+            pieces = chunks if i == 0 else [(0, 4), (4, 8)]
+            for lo, up in pieces:
+                cols = slice(lo * P, up * P)
+                acc = bank([P, (up - lo) * P])
                 nc.tensor.matmul_mx(
                     out=acc[:],
                     lhsT=v2_words[g][:, P * c : P * (c + 1)].bitcast(FP8X4),
                     lhsT_scale=v2_scales[:, P * i : P * (i + 1)],
-                    rhs=h_codes[:, 512 * n : 512 * (n + 1)].bitcast(FP8X4),
-                    rhs_scale=h_scales[:, 512 * n : 512 * (n + 1)],
+                    rhs=h_codes[:, cols].bitcast(FP8X4),
+                    rhs_scale=h_scales[:, cols],
                     start=True,
                     stop=True,
                 )
-                nc.scalar.copy(e[:, 512 * n : 512 * (n + 1)], acc[:])
+                nc.scalar.copy(e[:, cols], acc[:])
             return e
 
         def pod_side(i, e):

@@ -23,6 +23,7 @@ TILES = S // P
 MT = S2 // P
 SUMMED_FIRST = (0, 1, 2, 7)
 HELD_BACK = (5, 6)
+OFFLOADED = 5
 
 
 def tile_list_orchid_cross_scores_kernel(
@@ -60,9 +61,9 @@ def tile_list_orchid_cross_scores_kernel(
         stand_sb = held("stand_sb", [P, MT], F32)
 
         nc.gpsimd.memset(w4s_sb[:].rearrange("p a c -> p (a c)").bitcast(I32), 0)
-        make_identity(nc, ident[:])
         for q in range(4):
-            nc.vector.memset(tabs_sb[32 * q : 32 * q + 24, :].bitcast(I32), 0)
+            eng = nc.gpsimd if q >= 2 else nc.vector
+            eng.memset(tabs_sb[32 * q : 32 * q + 24, :].bitcast(I32), 0)
         nc.vector.memset(v_scales[0][:].bitcast(I32), 0)
 
         def load_weight_scales(queue, dst, src):
@@ -107,12 +108,13 @@ def tile_list_orchid_cross_scores_kernel(
 
         shift(0)
         load_words(tab_sb[1][:], tab_words[1])
-        nc.vector.memset(v_scales[1][:].bitcast(I32), 0)
+        nc.gpsimd.memset(v_scales[1][:].bitcast(I32), 0)
         shift(1)
 
-        nc.vector.memset(w8s_sb[:].rearrange("p a c -> p (a c)").bitcast(I32), 0)
+        nc.gpsimd.memset(w8s_sb[:].rearrange("p a c -> p (a c)").bitcast(I32), 0)
         for lo, up in ((0, 16), (32, 64), (64, 128)):
-            nc.vector.memset(tab2s_sb[lo:up, :].bitcast(I32), 0)
+            nc.gpsimd.memset(tab2s_sb[lo:up, :].bitcast(I32), 0)
+        make_identity(nc, ident[:])
 
         nc.sync.dma_start(
             out=w8_sb[:], in_=w8_words.rearrange("a p c i -> p a (c i)").bitcast(I32)
@@ -290,7 +292,7 @@ def tile_list_orchid_cross_scores_kernel(
             gather_v2(g)
 
         def scores(i):
-            e = ring.tile([P, S], F32, name="e")
+            e = ring.tile([P, S], F32, name="e", bufs=4)
             g, c = divmod(i, 2)
             pieces = chunks if i == 0 else [(0, 4), (4, 8)]
             for lo, up in pieces:
@@ -311,19 +313,47 @@ def tile_list_orchid_cross_scores_kernel(
         def pod_side(i, e):
             picked = ring.tile([P, NP], F32, name="picked")
             nc.vector.tensor_copy(picked[:], e[:].indirect(pos1_sb[:]))
-            pod = ring.tile([P, NP], F32, name="pod")
+            pod = ring.tile([P, NP], F32, name="pod", bufs=MT)
             nc.scalar.activation(pod[:], picked[:], ACT.Abs, bias=stand_sb[:, i : i + 1], scale=-1.0)
             return pod
 
-        es = [scores(0), scores(1)]
+        es = [scores(0), scores(1), scores(2)]
         pods = [pod_side(0, es[0])]
+        pollens = []
+        excess = {}
+
+        def difference(i):
+            diff = ring.tile([P, NP], F32, name="diff", bufs=2)
+            nc.gpsimd.tensor_tensor(diff[:], pods[i][:], pollens[i][:], ALU.subtract)
+            return diff
+
+        def lifted(i, diff):
+            gap = keep.tile([P, NP], F32, name="gap", tag="gap")
+            nc.scalar.activation(gap[:], diff[:], ACT.Relu)
+            res = ring.tile([P, NP], F32, name="res")
+            nc.gpsimd.tensor_tensor(res[:], pollens[i][:], gap[:], ALU.add)
+            nc.sync.dma_start(out=out[P * i : P * (i + 1), :], in_=res[:])
+
         for i in range(MT):
-            pollen = ring.tile([P, NP], F32, name="pollen")
+            pollen = ring.tile([P, NP], F32, name="pollen", bufs=MT)
             nc.vector.tensor_copy(pollen[:], es[i][:].indirect(pos2_sb[:]))
-            if i + 2 < MT:
-                es.append(scores(i + 2))
+            pollens.append(pollen)
             if i + 1 < MT:
                 pods.append(pod_side(i + 1, es[i + 1]))
-            res = ring.tile([P, NP], F32, name="res")
-            nc.vector.tensor_tensor(res[:], pods[i][:], pollen[:], ALU.max)
-            nc.sync.dma_start(out=out[P * i : P * (i + 1), :], in_=res[:])
+            if i < OFFLOADED:
+                excess[i] = difference(i)
+            if i == 0:
+                lifted(0, excess[0])
+            elif 2 <= i <= OFFLOADED:
+                lifted(i - 1, excess[i - 1])
+            if i + 3 < MT:
+                es.append(scores(i + 3))
+        last = keep.tile([P, (MT - OFFLOADED) * NP], F32, name="last", tag="gap")
+        for i in range(OFFLOADED, MT):
+            parts = 2 if i == MT - 1 else 1
+            width = NP // parts
+            for n in range(parts):
+                cols = slice(n * width, (n + 1) * width)
+                lo = (i - OFFLOADED) * NP + n * width
+                nc.vector.tensor_tensor(last[:, lo : lo + width], pods[i][:, cols], pollens[i][:, cols], ALU.max)
+                nc.sync.dma_start(out=out[P * i : P * (i + 1), cols], in_=last[:, lo : lo + width])

@@ -21,9 +21,9 @@ P = 128
 PASSES = K // 512
 TILES = S // P
 MT = S2 // P
-SUMMED_FIRST = (0, 1, 2, 7)
+SUMMED_FIRST = (0, 1, 7)
 HELD_BACK = (5, 6)
-OFFLOADED = 5
+OFFLOADED = 3
 
 
 def tile_list_orchid_cross_scores_kernel(
@@ -286,7 +286,7 @@ def tile_list_orchid_cross_scores_kernel(
             if j not in SUMMED_FIRST:
                 lows[j] = low(j)
         gather_v2(0)
-        for j in (0, 1, 3, 2, 4, 5, 6, 7):
+        for j in (0, 2, 1, 3, 4, 5, 6, 7):
             turn(j)
         for g in range(1, 4):
             gather_v2(g)

from contextlib import ExitStack

import concourse.mybir as mybir
from concourse.masks import make_identity

K, H, T, S, T3, S2, NP = 1024, 512, 4096, 1024, 2048, 1024, 512
FLOPS = 2 * (3 * K * H * S + H * S2 * S)

F32 = mybir.dt.float32
BF16 = mybir.dt.bfloat16
I32 = mybir.dt.int32
U32 = mybir.dt.uint32
U16 = mybir.dt.uint16
U8 = mybir.dt.uint8
FP8X4 = mybir.dt.float8_e4m3fn_x4
FP4X4 = mybir.dt.float4_e2m1fn_x4
ALU = mybir.AluOpType
ACT = mybir.ActivationFunctionType

P = 128
PASSES = K // 512
TILES = S // P
MT = S2 // P
SUMMED_FIRST = (0, 1, 7)
HELD_BACK = (5, 6)
OFFLOADED = 3


def tile_list_orchid_cross_scores_kernel(
    tc, tab_words, tab_scales, tab2_words, tab2_scales, offs, offs2, pos1, pos2,
    w1, w4_words, w4_scales, w8_words, w8_scales, stand, out,
):
    nc = tc.nc
    with ExitStack() as ctx:
        lists = ctx.enter_context(tc.tile_pool(name="lists", bufs=1))
        keep = ctx.enter_context(tc.tile_pool(name="keep", bufs=1))
        ring = ctx.enter_context(tc.tile_pool(name="ring", bufs=3))
        psum = ctx.enter_context(tc.psum_pool(name="psum", bufs=8))

        def held(name, shape, dtype):
            return keep.tile(shape, dtype, name=name, tag=name, align_bytes=64)

        def bank(shape):
            return psum.tile(shape, F32, name="bank")

        offs_sb = lists.tile([P, S // 16], U16, name="offs_sb")
        offs2_sb = lists.tile([P, S2 // 16], U16, name="offs2_sb")
        pos1_sb = lists.tile([P, NP // 16], U16, name="pos1_sb")
        pos2_sb = lists.tile([P, NP // 16], U16, name="pos2_sb")

        tab_sb = [held("tab%d" % a, [P, T], I32) for a in range(PASSES)]
        tabs_sb = held("tabs", [P, T], U8)
        tab2_sb = held("tab2", [P, T3], I32)
        tab2s_sb = held("tab2s", [P, T3], U8)
        w4_sb = held("w4", [P, PASSES, 2 * H], U8)
        w4s_sb = held("w4s", [P, PASSES, H], U8)
        w8_sb = held("w8", [P, PASSES, H], I32)
        w8s_sb = held("w8s", [P, PASSES, H], U8)
        v_scales = [held("vs%d" % a, [P, S], U8) for a in range(PASSES)]
        ident = held("ident", [P, P], F32)
        stand_sb = held("stand_sb", [P, MT], F32)

        nc.gpsimd.memset(w4s_sb[:].rearrange("p a c -> p (a c)").bitcast(I32), 0)
        for q in range(4):
            eng = nc.gpsimd if q >= 2 else nc.vector
            eng.memset(tabs_sb[32 * q : 32 * q + 24, :].bitcast(I32), 0)
        nc.vector.memset(v_scales[0][:].bitcast(I32), 0)

        def load_weight_scales(queue, dst, src):
            for q in range(4):
                queue.dma_start(
                    out=dst[32 * q : 32 * q + 4, :, :].bitcast(I32),
                    in_=src[:, 4 * q : 4 * q + 4, :].bitcast(I32).rearrange("a r c -> r a c"),
                )

        def load_words(dst, src):
            nc.sync.dma_start(out=dst, in_=src.rearrange("p n i -> p (n i)").bitcast(I32))

        half = H // 2
        w1_raw = [held("w1raw%d" % c, [P, 4, half], F32) for c in range(2 * PASSES)]

        def load_w1(c):
            a, hc = divmod(c, 2)
            nc.sync.dma_start(
                out=w1_raw[c][:],
                in_=w1[512 * a : 512 * (a + 1), hc * half : (hc + 1) * half].rearrange("(p i) c -> p i c", i=4),
            )

        nc.sync.dma_start(offs_sb[:], offs)
        for q in range(4):
            nc.sync.dma_start(
                out=tabs_sb[32 * q + 24 : 32 * q + 32, :].bitcast(I32),
                in_=tab_scales[:, 4 * q : 4 * q + 4, :].bitcast(I32),
            )
        nc.sync.dma_start(out=tab2s_sb[16:32, :].bitcast(I32), in_=tab2_scales[0].bitcast(I32))
        nc.sync.dma_start(offs2_sb[:], offs2)
        load_words(tab_sb[0][:], tab_words[0])
        nc.sync.dma_start(out=w4_sb[:].bitcast(I32), in_=w4_words.bitcast(I32).rearrange("a p c -> p a c"))
        load_weight_scales(nc.sync, w4s_sb, w4_scales)

        vs_picked = held("vs_picked", [P, S], U8)
        nc.vector.tensor_copy(vs_picked[:], tabs_sb[:].indirect(offs_sb[:]))

        def shift(a):
            nc.sync.dma_start(
                out=v_scales[a][0:100, :].bitcast(I32), in_=vs_picked[24 + 4 * a : 124 + 4 * a, :].bitcast(I32)
            )

        shift(0)
        load_words(tab_sb[1][:], tab_words[1])
        nc.gpsimd.memset(v_scales[1][:].bitcast(I32), 0)
        shift(1)

        nc.gpsimd.memset(w8s_sb[:].rearrange("p a c -> p (a c)").bitcast(I32), 0)
        for lo, up in ((0, 16), (32, 64), (64, 128)):
            nc.gpsimd.memset(tab2s_sb[lo:up, :].bitcast(I32), 0)
        make_identity(nc, ident[:])

        nc.sync.dma_start(
            out=w8_sb[:], in_=w8_words.rearrange("a p c i -> p a (c i)").bitcast(I32)
        )
        load_weight_scales(nc.sync, w8s_sb, w8_scales)
        for c in range(2 * PASSES):
            load_w1(c)
        load_words(tab2_sb[:], tab2_words[0])
        nc.sync.dma_start(pos1_sb[:], pos1)
        nc.sync.dma_start(pos2_sb[:], pos2)
        with nc.allow_non_contiguous_dma(reason="one reference score a partition"):
            nc.sync.dma_start(out=stand_sb[:], in_=stand.rearrange("(c p) -> p c", p=P))

        v_words = [[held("v%d_%d" % (a, g), [P, 512], U32) for g in range(2)] for a in range(PASSES)]

        def gather_v(a, g):
            nc.vector.tensor_copy(
                v_words[a][g][:], tab_sb[a][:].bitcast(U32).indirect(offs_sb[:, 32 * g : 32 * (g + 1)])
            )

        def first_stage(acc, j, a, rhs, rhs_scale):
            g, c = divmod(j, 4)
            nc.tensor.matmul_mx(
                out=acc[:],
                lhsT=v_words[a][g][:, P * c : P * (c + 1)].bitcast(FP8X4),
                lhsT_scale=v_scales[a][:, P * j : P * (j + 1)],
                rhs=rhs,
                rhs_scale=rhs_scale,
                start=(a == 0),
                stop=(a == PASSES - 1),
            )

        def dealt(j, ap):
            if j in SUMMED_FIRST:
                return ap.rearrange("p (m u e) -> p u m e", u=2, e=2)
            return ap.rearrange("p (m t) -> p t m", t=4)

        def as_dealt(j, ap):
            if j in SUMMED_FIRST:
                return ap.rearrange("p (u m e) -> p u m e", u=2, e=2)
            return ap.rearrange("p (t m) -> p t m", t=4)

        gather_v(0, 0)
        gather_v(0, 1)
        v2s_picked = held("v2s_picked", [P, S2], U8)
        nc.vector.tensor_copy(v2s_picked[:], tab2s_sb[:].indirect(offs2_sb[:]))

        a2_acc = [bank([P, H]) for j in range(TILES)]
        for j in range(TILES):
            first_stage(a2_acc[j], j, 0, w4_sb[:, 0, :].bitcast(FP4X4), w4s_sb[:, 0, :])
        gather_v(1, 0)
        gather_v(1, 1)
        a2 = [held("a2_%d" % j, [P, H], F32) for j in range(TILES)]
        for j in range(TILES):
            first_stage(a2_acc[j], j, 1, w4_sb[:, 1, :].bitcast(FP4X4), w4s_sb[:, 1, :])
            nc.scalar.copy(as_dealt(j, a2[j][:]), dealt(j, a2_acc[j][:]))

        w1_bf = keep.tile([P, PASSES * H, 4], BF16, name="w1bf", tag="reused", align_bytes=64)
        for c in range(2 * PASSES):
            dst = w1_bf[:, c * half : (c + 1) * half, :]
            src = w1_raw[c][:].rearrange("p i c -> p c i")
            if c < 2 * PASSES - 1:
                nc.gpsimd.tensor_scalar(dst, src, 1.0, 0.0, ALU.mult, ALU.add)
            else:
                nc.scalar.copy(dst, src)

        v2_scales = keep.tile([P, S2], U8, name="v2s", tag="w1raw3", align_bytes=64)
        nc.gpsimd.memset(v2_scales[:].bitcast(I32), 0)
        for q in range(4):
            nc.sync.dma_start(
                out=v2_scales[32 * q : 32 * q + 4, :].bitcast(I32),
                in_=v2s_picked[16 + 4 * q : 20 + 4 * q, :].bitcast(I32),
            )

        def high_product(j):
            acc = bank([P, H])
            for a in range(PASSES):
                first_stage(acc, j, a, w8_sb[:, a, :].bitcast(FP8X4), w8s_sb[:, a, :])
            return acc

        def high_max(j, acc, dst):
            nc.vector.tensor_tensor(as_dealt(j, dst), dealt(j, acc[:]), as_dealt(j, a2[j][:]), ALU.max)

        def high(j, dst):
            high_max(j, high_product(j), dst)

        hi = {}
        for j in range(TILES):
            if j not in HELD_BACK:
                hi[j] = held("hi_%d" % j, [P, H], F32)[:]
                high(j, hi[j])

        w1_codes = held("w1codes", [P, PASSES * H], U32)
        w1_scales = held("w1scales", [P, PASSES * H], U8)
        nc.vector.quantize_mx(
            out=w1_codes[:].bitcast(FP8X4), scales=w1_scales[:], in_=w1_bf[:].rearrange("p c i -> p (c i)")
        )
        hi_late = keep.tile([P, len(HELD_BACK) * H], F32, name="hi_late", tag="reused", align_bytes=64)
        for n, j in enumerate(HELD_BACK):
            hi[j] = hi_late[:, n * H : (n + 1) * H]
        late_acc = [high_product(j) for j in HELD_BACK]
        high_max(HELD_BACK[0], late_acc[0], hi[HELD_BACK[0]])

        v2_words = [held("v2w%d" % g, [P, 256], U32) for g in range(4)]

        def gather_v2(g):
            nc.vector.tensor_copy(
                v2_words[g][:], tab2_sb[:].bitcast(U32).indirect(offs2_sb[:, 16 * g : 16 * (g + 1)])
            )

        chunks = [(0, 4), (4, 6), (6, 7), (7, 8)]
        h_bf = [held("hbf%d" % lo, [P, (up - lo) * H], BF16) for lo, up in chunks]
        h_codes = held("hcodes", [P, S], U32)
        h_scales = held("hscales", [P, S], U8)

        def low(j):
            acc = bank([P, H])
            for a in range(PASSES):
                first_stage(acc, j, a, w1_codes[:, a * H : (a + 1) * H].bitcast(FP8X4), w1_scales[:, a * H : (a + 1) * H])
            dst = ring.tile([P, H], F32, name="low", bufs=TILES)
            nc.vector.tensor_tensor(as_dealt(j, dst[:]), dealt(j, acc[:]), as_dealt(j, a2[j][:]), ALU.min)
            return dst

        def add(j):
            ht = ring.tile([P, H], BF16, name="ht", bufs=len(SUMMED_FIRST))
            nc.gpsimd.tensor_tensor(ht[:], lows[j][:], hi[j], ALU.add)
            return ht

        done = []

        def turn(j):
            n = [c for c, (lo, up) in enumerate(chunks) if lo <= j < up][0]
            lo, up = chunks[n]
            dst = h_bf[n][:, (j - lo) * H : (j - lo + 1) * H]
            if j in SUMMED_FIRST:
                words = hts[j][:].bitcast(F32)
                turned = bank([P, 2, P])
                for u in range(2):
                    nc.tensor.transpose(turned[:, u, :], words[:, P * u : P * (u + 1)], ident[:])
                nc.scalar.copy(
                    dst.bitcast(F32).rearrange("p (j u) -> p j u", u=2), turned[:].rearrange("p u j -> p j u")
                )
            else:
                turned = bank([P, 4, P])
                for t in range(4):
                    cols = slice(P * t, P * (t + 1))
                    nc.tensor.matmul(
                        turned[:, t, :], hi[j][:, cols], ident[:], start=True, stop=False, is_transpose=True
                    )
                    nc.tensor.matmul(
                        turned[:, t, :], lows[j][:, cols], ident[:], start=False, stop=True, is_transpose=True
                    )
                nc.scalar.copy(dst.rearrange("p (j t) -> p j t", t=4), turned[:].rearrange("p t j -> p j t"))
            done.append(j)
            if all(x in done for x in range(lo, up)):
                nc.vector.quantize_mx(
                    out=h_codes[:, lo * P : up * P].bitcast(FP8X4),
                    scales=h_scales[:, lo * P : up * P],
                    in_=h_bf[n][:],
                )

        lows = {}
        hts = {}
        for j in SUMMED_FIRST:
            lows[j] = low(j)
            hts[j] = add(j)
        high_max(HELD_BACK[1], late_acc[1], hi[HELD_BACK[1]])
        for j in range(TILES):
            if j not in SUMMED_FIRST:
                lows[j] = low(j)
        gather_v2(0)
        for j in (0, 2, 1, 3, 4, 5, 6, 7):
            turn(j)
        for g in range(1, 4):
            gather_v2(g)

        def scores(i):
            e = ring.tile([P, S], F32, name="e", bufs=4)
            g, c = divmod(i, 2)
            pieces = chunks if i == 0 else [(0, 4), (4, 8)]
            for lo, up in pieces:
                cols = slice(lo * P, up * P)
                acc = bank([P, (up - lo) * P])
                nc.tensor.matmul_mx(
                    out=acc[:],
                    lhsT=v2_words[g][:, P * c : P * (c + 1)].bitcast(FP8X4),
                    lhsT_scale=v2_scales[:, P * i : P * (i + 1)],
                    rhs=h_codes[:, cols].bitcast(FP8X4),
                    rhs_scale=h_scales[:, cols],
                    start=True,
                    stop=True,
                )
                nc.scalar.copy(e[:, cols], acc[:])
            return e

        def pod_side(i, e):
            picked = ring.tile([P, NP], F32, name="picked")
            nc.vector.tensor_copy(picked[:], e[:].indirect(pos1_sb[:]))
            pod = ring.tile([P, NP], F32, name="pod", bufs=MT)
            nc.scalar.activation(pod[:], picked[:], ACT.Abs, bias=stand_sb[:, i : i + 1], scale=-1.0)
            return pod

        es = [scores(0), scores(1), scores(2)]
        pods = [pod_side(0, es[0])]
        pollens = []
        excess = {}

        def difference(i):
            diff = ring.tile([P, NP], F32, name="diff", bufs=2)
            nc.gpsimd.tensor_tensor(diff[:], pods[i][:], pollens[i][:], ALU.subtract)
            return diff

        def lifted(i, diff):
            gap = keep.tile([P, NP], F32, name="gap", tag="gap")
            nc.scalar.activation(gap[:], diff[:], ACT.Relu)
            res = ring.tile([P, NP], F32, name="res")
            nc.gpsimd.tensor_tensor(res[:], pollens[i][:], gap[:], ALU.add)
            nc.sync.dma_start(out=out[P * i : P * (i + 1), :], in_=res[:])

        for i in range(MT):
            pollen = ring.tile([P, NP], F32, name="pollen", bufs=MT)
            nc.vector.tensor_copy(pollen[:], es[i][:].indirect(pos2_sb[:]))
            pollens.append(pollen)
            if i + 1 < MT:
                pods.append(pod_side(i + 1, es[i + 1]))
            if i < OFFLOADED:
                excess[i] = difference(i)
            if i == 0:
                lifted(0, excess[0])
            elif 2 <= i <= OFFLOADED:
                lifted(i - 1, excess[i - 1])
            if i + 3 < MT:
                es.append(scores(i + 3))
        last = keep.tile([P, (MT - OFFLOADED) * NP], F32, name="last", tag="gap")
        for i in range(OFFLOADED, MT):
            parts = 2 if i == MT - 1 else 1
            width = NP // parts
            for n in range(parts):
                cols = slice(n * width, (n + 1) * width)
                lo = (i - OFFLOADED) * NP + n * width
                nc.vector.tensor_tensor(last[:, lo : lo + width], pods[i][:, cols], pollens[i][:, cols], ALU.max)
                nc.sync.dma_start(out=out[P * i : P * (i + 1), cols], in_=last[:, lo : lo + width])
